import numpy as np
import ml_dtypes


def mxq(x, axis, fmt="e4m3"):
    dtype, down = {"e4m3": (ml_dtypes.float8_e4m3fn, 7), "e5m2": (ml_dtypes.float8_e5m2, 14)}[fmt]
    v = np.moveaxis(np.asarray(x, np.float32).astype(ml_dtypes.bfloat16).astype(np.float64), axis, -1)
    blocks = v.reshape(v.shape[:-1] + (-1, 32))
    amax = np.abs(blocks).max(-1, keepdims=True)
    byte = np.maximum(np.where(amax > 0, np.frexp(amax)[1] - 1 + 127, 0) - down, 1)
    scale = np.exp2(byte - 127.0)
    codes = (blocks / scale).astype(np.float32).astype(dtype).astype(np.float64)
    return np.moveaxis((codes * scale).reshape(v.shape), -1, axis)


WIDE = False


def mx_kscale(k):
    if not WIDE:
        return np.ones(k)
    levels = np.array([10, -10, 5, -5, 0])
    if k % 512:
        return np.exp2(np.random.permutation(np.resize(levels, k // 32))).repeat(32)
    a = np.empty((k // 512, 16))
    for p in range(k // 512):
        a[p, :8] = np.random.permutation(np.resize(levels, 8))
        for g in range(8):
            far = levels[np.abs(levels - a[p, g]) >= 10]
            a[p, g + 8] = far[np.random.randint(len(far))]
    return np.exp2(a.ravel()).repeat(32)


BF16 = ml_dtypes.bfloat16


def bf(x):
    return np.asarray(x, np.float32).astype(BF16)


def f64(x):
    return np.asarray(x).astype(np.float64)


N, C = 512, 8192


def draw0():
    s = mx_kscale(N)
    h = np.random.standard_normal((N, N)) / np.sqrt(N)
    g = 1.0 + 0.1 * np.random.standard_normal(N)
    v = np.random.standard_normal(N) * 0.5
    x = np.random.standard_normal((N, C))
    return {"h": bf(h / s[None, :]), "g": bf(g * s), "v": bf(v), "x": bf(x)}


def core(h, g, v, x):
    h, g, v, x = f64(h), f64(g), f64(v), f64(x)
    c = 0.75
    e = 1.75
    a0 = -2.3
    s1 = e / (a0 - c)
    s2 = 1.0 / (2.0 / s1 - s1)
    u = v - c
    hq = mxq(h, 1, "e4m3")
    xg = g[:, None] * x
    p1 = hq @ mxq(xg, 0, "e4m3")
    y1 = (s1 / e) * (p1 + u[:, None] * x)
    yg = g[:, None] * y1
    p2 = hq @ mxq(yg, 0, "e4m3")
    y2 = (2.0 * s2 / e) * (p2 + u[:, None] * y1) - s1 * s2 * x
    return y2


def e4m3fn_bytes(y):
    return np.clip(np.asarray(y, np.float64), -448.0, 448.0).astype(np.float32).astype(ml_dtypes.float8_e4m3fn).view(np.uint8)


def e4m3fn_values(b):
    return np.asarray(b, np.uint8).view(ml_dtypes.float8_e4m3fn).astype(np.float64)


def setup_inputs():
    d = draw0()
    x0 = np.asarray(d['h']).astype(np.float64)
    s = (np.max(np.abs(x0), axis=(0,), keepdims=True) / 448.0).astype(np.float32)
    out = {}
    for k, v in d.items():
        if k == 'h':
            out['h_bytes'] = e4m3fn_bytes(x0 / s.astype(np.float64))
            out['h_scale'] = s
        else:
            out[k] = v
    return out


def reference(h_bytes, h_scale, g, v, x):
    return core(e4m3fn_values(h_bytes) * h_scale.astype(np.float64), g, v, x)

@@ -1,0 +1,216 @@
+from contextlib import ExitStack
+
+import concourse.mybir as mybir
+from concourse.masks import make_identity
+
+N, C = 512, 8192
+P = 128
+T = 4
+CW = 512
+CHUNKS = C // CW
+
+F32 = mybir.dt.float32
+BF16 = mybir.dt.bfloat16
+U32 = mybir.dt.uint32
+U8 = mybir.dt.uint8
+FP8 = mybir.dt.float8_e4m3fn
+FP8X4 = mybir.dt.float8_e4m3fn_x4
+ADD = mybir.AluOpType.add
+MULT = mybir.AluOpType.mult
+ACT_COPY = mybir.ActivationFunctionType.Copy
+
+CC = 0.75
+E = 1.75
+A0 = -2.3
+S1 = E / (A0 - CC)
+S2 = 1.0 / (2.0 / S1 - S1)
+A = S1 / E
+B = 2.0 * S2 / E
+
+FLOPS = 2 * 2 * N * N * C
+
+
+def tile_chebyshevfilteredsubspaceblock_t_kernel(tc, h_bytes, h_scale, g, v, x, out):
+    nc = tc.nc
+    x_view = x.rearrange("(p t) n -> p t n", t=T)
+    out_view = out.rearrange("(p t) n -> p t n", t=T)
+
+    with ExitStack() as ctx:
+        keep = ctx.enter_context(tc.tile_pool(name="keep", bufs=1))
+        xs = ctx.enter_context(tc.tile_pool(name="xs", bufs=4))
+        one = ctx.enter_context(tc.tile_pool(name="one", bufs=1))
+        two = ctx.enter_context(tc.tile_pool(name="two", bufs=2))
+        three = ctx.enter_context(tc.tile_pool(name="three", bufs=3))
+        psum = ctx.enter_context(tc.psum_pool(name="psum", bufs=4))
+
+        x_sb, xg_sb, xq, r_sb, cx_sb, p1, w_sb, yg_sb, ygi_sb, yq, p2, o_sb = ({} for i in range(12))
+
+        def load_x(c):
+            xt = xs.tile([P, T, CW], BF16)
+            nc.sync.dma_start(out=xt[:], in_=x_view[:, :, c * CW:(c + 1) * CW])
+            x_sb[c] = xt
+
+        ctx.enter_context(tc.manual_schedule())
+
+        hb = keep.tile([P, T, N], U8)
+        nc.sync.dma_start(out=hb[:], in_=h_bytes.rearrange("(m t) k -> m t k", t=T))
+        sc = keep.tile([P, N], F32)
+        nc.scalar.dma_start(out=sc[:], in_=h_scale.rearrange("o k -> (o k)").partition_broadcast(P))
+        gb = keep.tile([P, T], BF16)
+        vb = keep.tile([P, T], BF16)
+        nc.sync.dma_start(out=gb[:], in_=g.rearrange("(p t) -> p t", t=T))
+        nc.sync.dma_start(out=vb[:], in_=v.rearrange("(p t) -> p t", t=T))
+        for c in range(3):
+            load_x(c)
+
+        ident = keep.tile([P, P], F32)
+        make_identity(nc, ident[:])
+
+        u = keep.tile([P, T], F32)
+        ga = keep.tile([P, T], F32)
+        gau = keep.tile([P, T], F32)
+        bau = keep.tile([P, T], F32)
+        cxv = keep.tile([P, T], F32)
+        tmp = keep.tile([P, T], F32)
+        nc.vector.tensor_scalar(out=u[:], in0=vb[:], scalar1=-CC, scalar2=None, op0=ADD)
+        nc.vector.tensor_scalar(out=ga[:], in0=gb[:], scalar1=A, scalar2=None, op0=MULT)
+        nc.vector.tensor_scalar(out=bau[:], in0=u[:], scalar1=A * B, scalar2=None, op0=MULT)
+        nc.vector.tensor_tensor(out=gau[:], in0=ga[:], in1=u[:], op=MULT)
+        nc.vector.tensor_tensor(out=tmp[:], in0=bau[:], in1=u[:], op=MULT)
+        nc.vector.tensor_scalar(out=cxv[:], in0=tmp[:], scalar1=-S1 * S2, scalar2=None, op0=ADD)
+
+        def gain_x(c):
+            xgi = one.tile([P, CW, T], BF16, align_bytes=64)
+            for i in range(4):
+                cols = slice(i * CW // 4, (i + 1) * CW // 4)
+                nc.gpsimd.tensor_tensor(
+                    out=xgi[:, cols, :],
+                    in0=x_sb[c][:, :, cols].rearrange("p t n -> p n t"),
+                    in1=gb[:].unsqueeze(1).to_broadcast([P, CW // 4, T]),
+                    op=MULT,
+                )
+            xg_sb[c] = xgi
+
+        def quantize(src):
+            codes = two.tile([P, CW], U32, align_bytes=64)
+            scales = two.tile([P, CW], U8, align_bytes=64)
+            nc.vector.quantize_mx(out=codes[:].bitcast(FP8X4), scales=scales[:], in_=src[:].rearrange("p n t -> p (n t)"))
+            return codes, scales
+
+        def scale_r(c):
+            r = two.tile([P, T, CW], F32)
+            for t in range(T):
+                nc.scalar.activation(out=r[:, t, :], in_=x_sb[c][:, t, :], func=ACT_COPY, scale=gau[:, t:t + 1])
+            r_sb[c] = r
+
+        def scale_cx(c, ts):
+            if 0 in ts:
+                cx = two.tile([P, T, CW], F32)
+                cx_sb[c] = cx
+            for t in ts:
+                nc.scalar.activation(out=cx_sb[c][:, t, :], in_=x_sb[c][:, t, :], func=ACT_COPY, scale=cxv[:, t:t + 1])
+
+        def product(q, p_dict, c):
+            codes, scales = q
+            res = []
+            for t in range(T):
+                if p_dict is p1:
+                    acc1 = psum.tile([P, CW], F32)
+                    acc = acc1
+                else:
+                    acc2 = psum.tile([P, CW], F32)
+                    acc = acc2
+                nc.tensor.matmul_mx(
+                    out=acc[:],
+                    lhsT=h_codes[:, t * P:(t + 1) * P].bitcast(FP8X4),
+                    lhsT_scale=h_scales[:, t * P:(t + 1) * P],
+                    rhs=codes[:].bitcast(FP8X4),
+                    rhs_scale=scales[:],
+                    start=True,
+                    stop=True,
+                )
+                res.append(acc)
+            p_dict[c] = res
+
+        def stage_b(c):
+            yg = two.tile([P, T, CW], BF16)
+            for t in range(T):
+                nc.vector.scalar_tensor_tensor(
+                    out=yg[:, t, :], in0=p1[c][t][:], scalar=ga[:, t:t + 1], in1=r_sb[c][:, t, :], op0=MULT, op1=ADD)
+            yg_sb[c] = yg
+
+        def stage_w(c):
+            w = two.tile([P, T, CW], F32)
+            for t in range(T):
+                nc.vector.scalar_tensor_tensor(
+                    out=w[:, t, :], in0=p1[c][t][:], scalar=bau[:, t:t + 1], in1=cx_sb[c][:, t, :], op0=MULT, op1=ADD)
+            w_sb[c] = w
+
+        def stage_d(c):
+            o = three.tile([P, T, CW], F32)
+            for t in range(T):
+                nc.vector.scalar_tensor_tensor(
+                    out=o[:, t, :], in0=p2[c][t][:], scalar=B, in1=w_sb[c][:, t, :], op0=MULT, op1=ADD)
+                if c == CHUNKS - 1:
+                    nc.sync.dma_start(out=out_view[:, t:t + 1, c * CW:(c + 1) * CW], in_=o[:, t:t + 1, :])
+            if c < CHUNKS - 1:
+                nc.sync.dma_start(out=out_view[:, :, c * CW:(c + 1) * CW], in_=o[:])
+
+        def interleave(c):
+            ygi = two.tile([P, CW, T], BF16, align_bytes=64)
+            nc.scalar.copy(
+                out=ygi[:].rearrange("p (n i) t -> p n t i", i=4),
+                in_=yg_sb[c][:].rearrange("p t (n i) -> p n t i", i=4))
+            ygi_sb[c] = ygi
+
+        hf = keep.tile([P, T, N], BF16, align_bytes=64)
+        for t in range(T):
+            nc.vector.tensor_tensor(out=hf[:, t, :], in0=hb[:, t, :].bitcast(FP8), in1=sc[:], op=MULT)
+        hg = keep.tile([P, N, T], BF16, align_bytes=64)
+        hg_words = hg[:].rearrange("p n t -> p (n t)").bitcast(F32).rearrange("p (t m u) -> p t m u", t=T, u=2)
+        gain_x(0)
+        for i in range(2):
+            acc2 = psum.tile([P, CW], F32)
+            bank = acc2[:].rearrange("p (t u m) -> p t u m", t=2, u=2)
+            for j in range(2):
+                words = hf[:, 2 * i + j, :].bitcast(F32)
+                for k in range(2):
+                    nc.tensor.transpose(bank[:, j, k, :], words[:, k::2], ident[:])
+            if i == 0:
+                nc.vector.tensor_copy(out=hg_words[:, 2 * i:2 * i + 2], in_=bank.rearrange("p t u m -> p t m u"))
+            else:
+                nc.scalar.copy(out=hg_words[:, 2 * i:2 * i + 2], in_=bank.rearrange("p t u m -> p t m u"))
+        xq[0] = quantize(xg_sb[0])
+        h_codes = keep.tile([P, N], U32, align_bytes=64)
+        h_scales = keep.tile([P, N], U8, align_bytes=64)
+        nc.vector.quantize_mx(out=h_codes[:].bitcast(FP8X4), scales=h_scales[:], in_=hg[:].rearrange("p n t -> p (n t)"))
+        product(xq[0], p1, 0)
+        gain_x(1)
+        scale_r(0)
+        scale_cx(0, [0, 1, 2, 3])
+
+        for s in range(CHUNKS + 1):
+            if s + 3 < CHUNKS:
+                load_x(s + 3)
+            if s >= 1:
+                yq[s - 1] = quantize(ygi_sb[s - 1])
+                product(yq[s - 1], p2, s - 1)
+            if s + 1 < CHUNKS:
+                xq[s + 1] = quantize(xg_sb[s + 1])
+            if s + 2 < CHUNKS:
+                gain_x(s + 2)
+            if s < CHUNKS:
+                stage_b(s)
+            if s + 1 < CHUNKS:
+                scale_r(s + 1)
+                scale_cx(s + 1, [0, 1])
+            if s < CHUNKS:
+                interleave(s)
+            if s + 1 < CHUNKS:
+                scale_cx(s + 1, [2, 3])
+            if s >= 1:
+                stage_d(s - 1)
+            if s < CHUNKS:
+                stage_w(s)
+            if s + 1 < CHUNKS:
+                product(xq[s + 1], p1, s + 1)

@@ -8,6 +8,7 @@ P = 128
 T = 4
 CW = 512
 CHUNKS = C // CW
+POOL_W = 1
 
 F32 = mybir.dt.float32
 BF16 = mybir.dt.bfloat16
@@ -38,12 +39,11 @@ def tile_chebyshevfilteredsubspaceblock_t_kernel(tc, h_bytes, h_scale, g, v, x, 
     with ExitStack() as ctx:
         keep = ctx.enter_context(tc.tile_pool(name="keep", bufs=1))
         xs = ctx.enter_context(tc.tile_pool(name="xs", bufs=4))
-        one = ctx.enter_context(tc.tile_pool(name="one", bufs=1))
         two = ctx.enter_context(tc.tile_pool(name="two", bufs=2))
         three = ctx.enter_context(tc.tile_pool(name="three", bufs=3))
         psum = ctx.enter_context(tc.psum_pool(name="psum", bufs=4))
 
-        x_sb, xg_sb, xq, r_sb, cx_sb, p1, w_sb, yg_sb, ygi_sb, yq, p2, o_sb = ({} for i in range(12))
+        x_sb, pair_sb, xq, r_sb, cx_sb, p1, w_sb, yg_sb, yq, p2, q_sb = ({} for i in range(11))
 
         def load_x(c):
             xt = xs.tile([P, T, CW], BF16)
@@ -80,22 +80,28 @@ def tile_chebyshevfilteredsubspaceblock_t_kernel(tc, h_bytes, h_scale, g, v, x, 
         nc.vector.tensor_scalar(out=cxv[:], in0=tmp[:], scalar1=-S1 * S2, scalar2=None, op0=ADD)
 
         def gain_x(c):
-            xgi = one.tile([P, CW, T], BF16, align_bytes=64)
+            pair = two.tile([P, 2, CW, T], BF16, align_bytes=64)
+            pair_sb[c - 1] = pair
             for i in range(4):
                 cols = slice(i * CW // 4, (i + 1) * CW // 4)
                 nc.gpsimd.tensor_tensor(
-                    out=xgi[:, cols, :],
+                    out=pair[:, 0, cols, :],
                     in0=x_sb[c][:, :, cols].rearrange("p t n -> p n t"),
                     in1=gb[:].unsqueeze(1).to_broadcast([P, CW // 4, T]),
                     op=MULT,
                 )
-            xg_sb[c] = xgi
 
-        def quantize(src):
-            codes = two.tile([P, CW], U32, align_bytes=64)
-            scales = two.tile([P, CW], U8, align_bytes=64)
-            nc.vector.quantize_mx(out=codes[:].bitcast(FP8X4), scales=scales[:], in_=src[:].rearrange("p n t -> p (n t)"))
-            return codes, scales
+        def quantize(s):
+            codes = two.tile([P, 2, CW], U32, align_bytes=64)
+            scales = two.tile([P, 2, CW], U8, align_bytes=64)
+            lo = 0 if s + 1 < CHUNKS else 1
+            hi = 2 if s >= 1 else 1
+            nc.vector.quantize_mx(
+                out=codes[:, lo:hi, :].rearrange("p h n -> p (h n)").bitcast(FP8X4),
+                scales=scales[:, lo:hi, :].rearrange("p h n -> p (h n)"),
+                in_=pair_sb[s][:, lo:hi].rearrange("p h n t -> p (h n t)"))
+            xq[s + 1] = codes[:, 0, :], scales[:, 0, :]
+            yq[s - 1] = codes[:, 1, :], scales[:, 1, :]
 
         def scale_r(c):
             r = two.tile([P, T, CW], F32)
@@ -124,8 +130,8 @@ def tile_chebyshevfilteredsubspaceblock_t_kernel(tc, h_bytes, h_scale, g, v, x, 
                     out=acc[:],
                     lhsT=h_codes[:, t * P:(t + 1) * P].bitcast(FP8X4),
                     lhsT_scale=h_scales[:, t * P:(t + 1) * P],
-                    rhs=codes[:].bitcast(FP8X4),
-                    rhs_scale=scales[:],
+                    rhs=codes.bitcast(FP8X4),
+                    rhs_scale=scales,
                     start=True,
                     stop=True,
                 )
@@ -140,11 +146,24 @@ def tile_chebyshevfilteredsubspaceblock_t_kernel(tc, h_bytes, h_scale, g, v, x, 
             yg_sb[c] = yg
 
         def stage_w(c):
-            w = two.tile([P, T, CW], F32)
-            for t in range(T):
+            w = w_sb[c]
+            for t in range(T - POOL_W):
                 nc.vector.scalar_tensor_tensor(
                     out=w[:, t, :], in0=p1[c][t][:], scalar=bau[:, t:t + 1], in1=cx_sb[c][:, t, :], op0=MULT, op1=ADD)
+
+        def stage_q(c):
+            w = two.tile([P, T, CW], F32)
             w_sb[c] = w
+            q = two.tile([P, POOL_W, CW], F32)
+            q_sb[c] = q
+            for j in range(POOL_W):
+                t = T - POOL_W + j
+                nc.scalar.activation(out=q[:, j, :], in_=p1[c][t][:], func=ACT_COPY, scale=bau[:, t:t + 1])
+
+        def stage_pool_w(c):
+            for j in range(POOL_W):
+                t = T - POOL_W + j
+                nc.gpsimd.tensor_tensor(out=w_sb[c][:, t, :], in0=q_sb[c][:, j, :], in1=cx_sb[c][:, t, :], op=ADD)
 
         def stage_d(c):
             o = three.tile([P, T, CW], F32)
@@ -157,11 +176,12 @@ def tile_chebyshevfilteredsubspaceblock_t_kernel(tc, h_bytes, h_scale, g, v, x, 
                 nc.sync.dma_start(out=out_view[:, :, c * CW:(c + 1) * CW], in_=o[:])
 
         def interleave(c):
-            ygi = two.tile([P, CW, T], BF16, align_bytes=64)
+            if c + 1 not in pair_sb:
+                pair = two.tile([P, 2, CW, T], BF16, align_bytes=64)
+                pair_sb[c + 1] = pair
             nc.scalar.copy(
-                out=ygi[:].rearrange("p (n i) t -> p n t i", i=4),
+                out=pair_sb[c + 1][:, 1].rearrange("p (n i) t -> p n t i", i=4),
                 in_=yg_sb[c][:].rearrange("p t (n i) -> p n t i", i=4))
-            ygi_sb[c] = ygi
 
         hf = keep.tile([P, T, N], BF16, align_bytes=64)
         for t in range(T):
@@ -180,7 +200,7 @@ def tile_chebyshevfilteredsubspaceblock_t_kernel(tc, h_bytes, h_scale, g, v, x, 
                 nc.vector.tensor_copy(out=hg_words[:, 2 * i:2 * i + 2], in_=bank.rearrange("p t u m -> p t m u"))
             else:
                 nc.scalar.copy(out=hg_words[:, 2 * i:2 * i + 2], in_=bank.rearrange("p t u m -> p t m u"))
-        xq[0] = quantize(xg_sb[0])
+        quantize(-1)
         h_codes = keep.tile([P, N], U32, align_bytes=64)
         h_scales = keep.tile([P, N], U8, align_bytes=64)
         nc.vector.quantize_mx(out=h_codes[:].bitcast(FP8X4), scales=h_scales[:], in_=hg[:].rearrange("p n t -> p (n t)"))
@@ -192,14 +212,14 @@ def tile_chebyshevfilteredsubspaceblock_t_kernel(tc, h_bytes, h_scale, g, v, x, 
         for s in range(CHUNKS + 1):
             if s + 3 < CHUNKS:
                 load_x(s + 3)
+            quantize(s)
             if s >= 1:
-                yq[s - 1] = quantize(ygi_sb[s - 1])
                 product(yq[s - 1], p2, s - 1)
-            if s + 1 < CHUNKS:
-                xq[s + 1] = quantize(xg_sb[s + 1])
             if s + 2 < CHUNKS:
                 gain_x(s + 2)
             if s < CHUNKS:
+                stage_q(s)
+                stage_pool_w(s)
                 stage_b(s)
             if s + 1 < CHUNKS:
                 scale_r(s + 1)

@@ -9,6 +9,7 @@ T = 4
 CW = 512
 CHUNKS = C // CW
 POOL_W = 1
+R_ACT = 2
 
 F32 = mybir.dt.float32
 BF16 = mybir.dt.bfloat16
@@ -38,12 +39,12 @@ def tile_chebyshevfilteredsubspaceblock_t_kernel(tc, h_bytes, h_scale, g, v, x, 
 
     with ExitStack() as ctx:
         keep = ctx.enter_context(tc.tile_pool(name="keep", bufs=1))
-        xs = ctx.enter_context(tc.tile_pool(name="xs", bufs=4))
+        xs = ctx.enter_context(tc.tile_pool(name="xs", bufs=5))
         two = ctx.enter_context(tc.tile_pool(name="two", bufs=2))
         three = ctx.enter_context(tc.tile_pool(name="three", bufs=3))
         psum = ctx.enter_context(tc.psum_pool(name="psum", bufs=4))
 
-        x_sb, pair_sb, xq, r_sb, cx_sb, p1, w_sb, yg_sb, yq, p2, q_sb = ({} for i in range(11))
+        x_sb, pair_sb, xq, r_sb, cx_sb, p1, w_sb, yg_sb, yq, p2, q_sb, xg_ps = ({} for i in range(12))
 
         def load_x(c):
             xt = xs.tile([P, T, CW], BF16)
@@ -52,15 +53,16 @@ def tile_chebyshevfilteredsubspaceblock_t_kernel(tc, h_bytes, h_scale, g, v, x, 
 
         ctx.enter_context(tc.manual_schedule())
 
-        hb = keep.tile([P, T, N], U8)
-        nc.sync.dma_start(out=hb[:], in_=h_bytes.rearrange("(m t) k -> m t k", t=T))
         sc = keep.tile([P, N], F32)
         nc.scalar.dma_start(out=sc[:], in_=h_scale.rearrange("o k -> (o k)").partition_broadcast(P))
         gb = keep.tile([P, T], BF16)
         vb = keep.tile([P, T], BF16)
         nc.sync.dma_start(out=gb[:], in_=g.rearrange("(p t) -> p t", t=T))
         nc.sync.dma_start(out=vb[:], in_=v.rearrange("(p t) -> p t", t=T))
-        for c in range(3):
+        load_x(0)
+        hb = keep.tile([P, T, N], U8)
+        nc.sync.dma_start(out=hb[:], in_=h_bytes.rearrange("(m t) k -> m t k", t=T))
+        for c in range(1, 4):
             load_x(c)
 
         ident = keep.tile([P, P], F32)
@@ -79,17 +81,38 @@ def tile_chebyshevfilteredsubspaceblock_t_kernel(tc, h_bytes, h_scale, g, v, x, 
         nc.vector.tensor_tensor(out=tmp[:], in0=bau[:], in1=u[:], op=MULT)
         nc.vector.tensor_scalar(out=cxv[:], in0=tmp[:], scalar1=-S1 * S2, scalar2=None, op0=ADD)
 
-        def gain_x(c):
-            pair = two.tile([P, 2, CW, T], BF16, align_bytes=64)
-            pair_sb[c - 1] = pair
+        def pair_of(s):
+            if s not in pair_sb:
+                pair = two.tile([P, 2, CW, T], BF16, align_bytes=64)
+                pair_sb[s] = pair
+            return pair_sb[s]
+
+        def gain_x(c, engine):
+            pair = pair_of(c - 1)
             for i in range(4):
                 cols = slice(i * CW // 4, (i + 1) * CW // 4)
-                nc.gpsimd.tensor_tensor(
+                engine.tensor_tensor(
                     out=pair[:, 0, cols, :],
                     in0=x_sb[c][:, :, cols].rearrange("p t n -> p n t"),
                     in1=gb[:].unsqueeze(1).to_broadcast([P, CW // 4, T]),
                     op=MULT,
                 )
+
+        def gain_x_pe(c):
+            banks = []
+            for i in range(2):
+                cols = slice(i * CW // 2, (i + 1) * CW // 2)
+                acc2 = psum.tile([P, T, CW // 2], BF16)
+                for t in range(T):
+                    nc.tensor.matmul(out=acc2[:, t, :], lhsT=diag[:, t, :], rhs=x_sb[c][:, t, cols], start=True, stop=True)
+                banks.append(acc2)
+            xg_ps[c] = banks
+
+        def gain_x_out(c):
+            pair = pair_of(c - 1)
+            for i in range(2):
+                cols = slice(i * CW // 2, (i + 1) * CW // 2)
+                nc.scalar.copy(out=pair[:, 0, cols, :], in_=xg_ps[c][i][:].rearrange("p t n -> p n t"))
 
         def quantize(s):
             codes = two.tile([P, 2, CW], U32, align_bytes=64)
@@ -103,18 +126,25 @@ def tile_chebyshevfilteredsubspaceblock_t_kernel(tc, h_bytes, h_scale, g, v, x, 
             xq[s + 1] = codes[:, 0, :], scales[:, 0, :]
             yq[s - 1] = codes[:, 1, :], scales[:, 1, :]
 
-        def scale_r(c):
-            r = two.tile([P, T, CW], F32)
-            for t in range(T):
-                nc.scalar.activation(out=r[:, t, :], in_=x_sb[c][:, t, :], func=ACT_COPY, scale=gau[:, t:t + 1])
-            r_sb[c] = r
+        def times_x(out_ap, c, t, factor, on_pool):
+            if on_pool:
+                nc.gpsimd.tensor_scalar(out=out_ap, in0=x_sb[c][:, t, :], scalar1=factor[:, t:t + 1], scalar2=0.0, op0=MULT, op1=ADD)
+            else:
+                nc.scalar.activation(out=out_ap, in_=x_sb[c][:, t, :], func=ACT_COPY, scale=factor[:, t:t + 1])
 
-        def scale_cx(c, ts):
-            if 0 in ts:
+        def scale_r(c, ts, on_pool):
+            if c not in r_sb:
+                r = two.tile([P, T, CW], F32)
+                r_sb[c] = r
+            for t in ts:
+                times_x(r_sb[c][:, t, :], c, t, gau, on_pool)
+
+        def scale_cx(c, ts, on_pool):
+            if c not in cx_sb:
                 cx = two.tile([P, T, CW], F32)
                 cx_sb[c] = cx
             for t in ts:
-                nc.scalar.activation(out=cx_sb[c][:, t, :], in_=x_sb[c][:, t, :], func=ACT_COPY, scale=cxv[:, t:t + 1])
+                times_x(cx_sb[c][:, t, :], c, t, cxv, on_pool)
 
         def product(q, p_dict, c):
             codes, scales = q
@@ -176,19 +206,19 @@ def tile_chebyshevfilteredsubspaceblock_t_kernel(tc, h_bytes, h_scale, g, v, x, 
                 nc.sync.dma_start(out=out_view[:, :, c * CW:(c + 1) * CW], in_=o[:])
 
         def interleave(c):
-            if c + 1 not in pair_sb:
-                pair = two.tile([P, 2, CW, T], BF16, align_bytes=64)
-                pair_sb[c + 1] = pair
             nc.scalar.copy(
-                out=pair_sb[c + 1][:, 1].rearrange("p (n i) t -> p n t i", i=4),
+                out=pair_of(c + 1)[:, 1].rearrange("p (n i) t -> p n t i", i=4),
                 in_=yg_sb[c][:].rearrange("p t (n i) -> p n t i", i=4))
 
+        gain_x(0, nc.vector)
+        gain_x(1, nc.gpsimd)
+        gain_x(2, nc.gpsimd)
+        scale_r(0, range(T), False)
         hf = keep.tile([P, T, N], BF16, align_bytes=64)
         for t in range(T):
             nc.vector.tensor_tensor(out=hf[:, t, :], in0=hb[:, t, :].bitcast(FP8), in1=sc[:], op=MULT)
         hg = keep.tile([P, N, T], BF16, align_bytes=64)
         hg_words = hg[:].rearrange("p n t -> p (n t)").bitcast(F32).rearrange("p (t m u) -> p t m u", t=T, u=2)
-        gain_x(0)
         for i in range(2):
             acc2 = psum.tile([P, CW], F32)
             bank = acc2[:].rearrange("p (t u m) -> p t u m", t=2, u=2)
@@ -197,39 +227,48 @@ def tile_chebyshevfilteredsubspaceblock_t_kernel(tc, h_bytes, h_scale, g, v, x, 
                 for k in range(2):
                     nc.tensor.transpose(bank[:, j, k, :], words[:, k::2], ident[:])
             if i == 0:
+                quantize(-1)
                 nc.vector.tensor_copy(out=hg_words[:, 2 * i:2 * i + 2], in_=bank.rearrange("p t u m -> p t m u"))
             else:
                 nc.scalar.copy(out=hg_words[:, 2 * i:2 * i + 2], in_=bank.rearrange("p t u m -> p t m u"))
-        quantize(-1)
+        diag = keep.tile([P, T, P], BF16)
+        for t in range(T):
+            nc.vector.tensor_scalar(out=diag[:, t, :], in0=ident[:], scalar1=gb[:, t:t + 1], scalar2=None, op0=MULT)
         h_codes = keep.tile([P, N], U32, align_bytes=64)
         h_scales = keep.tile([P, N], U8, align_bytes=64)
         nc.vector.quantize_mx(out=h_codes[:].bitcast(FP8X4), scales=h_scales[:], in_=hg[:].rearrange("p n t -> p (n t)"))
         product(xq[0], p1, 0)
-        gain_x(1)
-        scale_r(0)
-        scale_cx(0, [0, 1, 2, 3])
+        scale_cx(0, range(T), False)
 
         for s in range(CHUNKS + 1):
-            if s + 3 < CHUNKS:
-                load_x(s + 3)
+            early = s < 2
+            if s + 4 < CHUNKS:
+                load_x(s + 4)
             quantize(s)
             if s >= 1:
                 product(yq[s - 1], p2, s - 1)
-            if s + 2 < CHUNKS:
-                gain_x(s + 2)
             if s < CHUNKS:
                 stage_q(s)
-                stage_pool_w(s)
-                stage_b(s)
+                if 4 <= s + 2 < CHUNKS:
+                    gain_x_out(s + 2)
             if s + 1 < CHUNKS:
-                scale_r(s + 1)
-                scale_cx(s + 1, [0, 1])
+                scale_r(s + 1, range(T) if early else range(R_ACT), False)
+                scale_r(s + 1, range(0) if early else range(R_ACT, T), True)
             if s < CHUNKS:
+                stage_pool_w(s)
+            if s + 1 < CHUNKS and not early:
+                scale_cx(s + 1, range(T), True)
+            if s == 0:
+                gain_x(3, nc.gpsimd)
+            if s < CHUNKS:
+                stage_b(s)
                 interleave(s)
-            if s + 1 < CHUNKS:
-                scale_cx(s + 1, [2, 3])
+            if s + 1 < CHUNKS and early:
+                scale_cx(s + 1, range(T), False)
             if s >= 1:
                 stage_d(s - 1)
+            if 4 <= s + 3 < CHUNKS:
+                gain_x_pe(s + 3)
             if s < CHUNKS:
                 stage_w(s)
             if s + 1 < CHUNKS:

@@ -8,8 +8,9 @@ P = 128
 T = 4
 CW = 512
 CHUNKS = C // CW
-POOL_W = 1
-R_ACT = 2
+POOL_W = (1, 2)
+R_ACT = 3
+PE_CHUNKS = (1,) + tuple(range(4, 15))
 
 F32 = mybir.dt.float32
 BF16 = mybir.dt.bfloat16
@@ -41,15 +42,21 @@ def tile_chebyshevfilteredsubspaceblock_t_kernel(tc, h_bytes, h_scale, g, v, x, 
         keep = ctx.enter_context(tc.tile_pool(name="keep", bufs=1))
         xs = ctx.enter_context(tc.tile_pool(name="xs", bufs=5))
         two = ctx.enter_context(tc.tile_pool(name="two", bufs=2))
+        four = ctx.enter_context(tc.tile_pool(name="four", bufs=4))
         three = ctx.enter_context(tc.tile_pool(name="three", bufs=3))
-        psum = ctx.enter_context(tc.psum_pool(name="psum", bufs=4))
+        psum = ctx.enter_context(tc.psum_pool(name="psum", bufs=1))
 
-        x_sb, pair_sb, xq, r_sb, cx_sb, p1, w_sb, yg_sb, yq, p2, q_sb, xg_ps = ({} for i in range(12))
+        x_sb, pair_sb, xq, r_sb, cx_sb, p1, w_sb, yg_sb, yq, p2, q_sb, xg_ps, code_sb = ({} for i in range(13))
 
         def load_x(c):
             xt = xs.tile([P, T, CW], BF16)
             nc.sync.dma_start(out=xt[:], in_=x_view[:, :, c * CW:(c + 1) * CW])
             x_sb[c] = xt
+
+        def load_last():
+            x_last = keep.tile([P, T, CW], BF16)
+            nc.sync.dma_start(out=x_last[:], in_=x_view[:, :, C - CW:])
+            x_sb[CHUNKS - 1] = x_last
 
         ctx.enter_context(tc.manual_schedule())
 
@@ -64,6 +71,7 @@ def tile_chebyshevfilteredsubspaceblock_t_kernel(tc, h_bytes, h_scale, g, v, x, 
         nc.sync.dma_start(out=hb[:], in_=h_bytes.rearrange("(m t) k -> m t k", t=T))
         for c in range(1, 4):
             load_x(c)
+        load_last()
 
         ident = keep.tile([P, P], F32)
         make_identity(nc, ident[:])
@@ -83,13 +91,13 @@ def tile_chebyshevfilteredsubspaceblock_t_kernel(tc, h_bytes, h_scale, g, v, x, 
 
         def pair_of(s):
             if s not in pair_sb:
-                pair = two.tile([P, 2, CW, T], BF16, align_bytes=64)
+                pair = four.tile([P, 2, CW, T], BF16, align_bytes=64)
                 pair_sb[s] = pair
             return pair_sb[s]
 
-        def gain_x(c, engine):
+        def gain_x(c, engine, pieces):
             pair = pair_of(c - 1)
-            for i in range(4):
+            for i in pieces:
                 cols = slice(i * CW // 4, (i + 1) * CW // 4)
                 engine.tensor_tensor(
                     out=pair[:, 0, cols, :],
@@ -102,10 +110,10 @@ def tile_chebyshevfilteredsubspaceblock_t_kernel(tc, h_bytes, h_scale, g, v, x, 
             banks = []
             for i in range(2):
                 cols = slice(i * CW // 2, (i + 1) * CW // 2)
-                acc2 = psum.tile([P, T, CW // 2], BF16)
+                bank = psum.tile([P, T, CW // 2], BF16, name=f"second_{i}")
                 for t in range(T):
-                    nc.tensor.matmul(out=acc2[:, t, :], lhsT=diag[:, t, :], rhs=x_sb[c][:, t, cols], start=True, stop=True)
-                banks.append(acc2)
+                    nc.tensor.matmul(out=bank[:, t, :], lhsT=diag[:, t, :], rhs=x_sb[c][:, t, cols], start=True, stop=True)
+                banks.append(bank)
             xg_ps[c] = banks
 
         def gain_x_out(c):
@@ -123,6 +131,7 @@ def tile_chebyshevfilteredsubspaceblock_t_kernel(tc, h_bytes, h_scale, g, v, x, 
                 out=codes[:, lo:hi, :].rearrange("p h n -> p (h n)").bitcast(FP8X4),
                 scales=scales[:, lo:hi, :].rearrange("p h n -> p (h n)"),
                 in_=pair_sb[s][:, lo:hi].rearrange("p h n t -> p (h n t)"))
+            code_sb[s] = codes[:, lo, 0:1]
             xq[s + 1] = codes[:, 0, :], scales[:, 0, :]
             yq[s - 1] = codes[:, 1, :], scales[:, 1, :]
 
@@ -146,16 +155,11 @@ def tile_chebyshevfilteredsubspaceblock_t_kernel(tc, h_bytes, h_scale, g, v, x, 
             for t in ts:
                 times_x(cx_sb[c][:, t, :], c, t, cxv, on_pool)
 
-        def product(q, p_dict, c):
+        def product(q, p_dict, c, kind):
             codes, scales = q
-            res = []
-            for t in range(T):
-                if p_dict is p1:
-                    acc1 = psum.tile([P, CW], F32)
-                    acc = acc1
-                else:
-                    acc2 = psum.tile([P, CW], F32)
-                    acc = acc2
+            res = {}
+            for t in reversed(range(T)):
+                acc = psum.tile([P, CW], F32, name=f"{kind}_{t}")
                 nc.tensor.matmul_mx(
                     out=acc[:],
                     lhsT=h_codes[:, t * P:(t + 1) * P].bitcast(FP8X4),
@@ -165,7 +169,7 @@ def tile_chebyshevfilteredsubspaceblock_t_kernel(tc, h_bytes, h_scale, g, v, x, 
                     start=True,
                     stop=True,
                 )
-                res.append(acc)
+                res[t] = acc
             p_dict[c] = res
 
         def stage_b(c):
@@ -177,22 +181,22 @@ def tile_chebyshevfilteredsubspaceblock_t_kernel(tc, h_bytes, h_scale, g, v, x, 
 
         def stage_w(c):
             w = w_sb[c]
-            for t in range(T - POOL_W):
+            for t in reversed(range(T - POOL_W[c % 2])):
                 nc.vector.scalar_tensor_tensor(
                     out=w[:, t, :], in0=p1[c][t][:], scalar=bau[:, t:t + 1], in1=cx_sb[c][:, t, :], op0=MULT, op1=ADD)
 
         def stage_q(c):
             w = two.tile([P, T, CW], F32)
             w_sb[c] = w
-            q = two.tile([P, POOL_W, CW], F32)
+            q = two.tile([P, POOL_W[c % 2], CW], F32)
             q_sb[c] = q
-            for j in range(POOL_W):
-                t = T - POOL_W + j
+            for j in reversed(range(POOL_W[c % 2])):
+                t = T - POOL_W[c % 2] + j
                 nc.scalar.activation(out=q[:, j, :], in_=p1[c][t][:], func=ACT_COPY, scale=bau[:, t:t + 1])
 
         def stage_pool_w(c):
-            for j in range(POOL_W):
-                t = T - POOL_W + j
+            for j in reversed(range(POOL_W[c % 2])):
+                t = T - POOL_W[c % 2] + j
                 nc.gpsimd.tensor_tensor(out=w_sb[c][:, t, :], in0=q_sb[c][:, j, :], in1=cx_sb[c][:, t, :], op=ADD)
 
         def stage_d(c):
@@ -210,66 +214,88 @@ def tile_chebyshevfilteredsubspaceblock_t_kernel(tc, h_bytes, h_scale, g, v, x, 
                 out=pair_of(c + 1)[:, 1].rearrange("p (n i) t -> p n t i", i=4),
                 in_=yg_sb[c][:].rearrange("p t (n i) -> p n t i", i=4))
 
-        gain_x(0, nc.vector)
-        gain_x(1, nc.gpsimd)
-        gain_x(2, nc.gpsimd)
-        scale_r(0, range(T), False)
+        gate = keep.tile([P, 1], U32)
+        diag = keep.tile([P, T, P], BF16)
+        gain_x(0, nc.vector, range(4))
         hf = keep.tile([P, T, N], BF16, align_bytes=64)
         for t in range(T):
             nc.vector.tensor_tensor(out=hf[:, t, :], in0=hb[:, t, :].bitcast(FP8), in1=sc[:], op=MULT)
+        for t in range(T):
+            nc.vector.tensor_scalar(out=diag[:, t, :], in0=ident[:], scalar1=gb[:, t:t + 1], scalar2=None, op0=MULT)
+        quantize(-1)
+        scale_r(0, range(T), False)
         hg = keep.tile([P, N, T], BF16, align_bytes=64)
         hg_words = hg[:].rearrange("p n t -> p (n t)").bitcast(F32).rearrange("p (t m u) -> p t m u", t=T, u=2)
         for i in range(2):
-            acc2 = psum.tile([P, CW], F32)
-            bank = acc2[:].rearrange("p (t u m) -> p t u m", t=2, u=2)
+            turned = psum.tile([P, CW], F32, name=f"second_{i + 2}")
+            bank = turned[:].rearrange("p (t u m) -> p t u m", t=2, u=2)
             for j in range(2):
                 words = hf[:, 2 * i + j, :].bitcast(F32)
                 for k in range(2):
                     nc.tensor.transpose(bank[:, j, k, :], words[:, k::2], ident[:])
             if i == 0:
-                quantize(-1)
                 nc.vector.tensor_copy(out=hg_words[:, 2 * i:2 * i + 2], in_=bank.rearrange("p t u m -> p t m u"))
             else:
                 nc.scalar.copy(out=hg_words[:, 2 * i:2 * i + 2], in_=bank.rearrange("p t u m -> p t m u"))
-        diag = keep.tile([P, T, P], BF16)
-        for t in range(T):
-            nc.vector.tensor_scalar(out=diag[:, t, :], in0=ident[:], scalar1=gb[:, t:t + 1], scalar2=None, op0=MULT)
         h_codes = keep.tile([P, N], U32, align_bytes=64)
         h_scales = keep.tile([P, N], U8, align_bytes=64)
         nc.vector.quantize_mx(out=h_codes[:].bitcast(FP8X4), scales=h_scales[:], in_=hg[:].rearrange("p n t -> p (n t)"))
-        product(xq[0], p1, 0)
+        gain_x_pe(1)
+        product(xq[0], p1, 0, "first")
+        gain_x_out(1)
         scale_cx(0, range(T), False)
+        nc.gpsimd.tensor_copy(out=gate[:], in_=h_codes[:, 0:1])
 
-        for s in range(CHUNKS + 1):
+        pair_last = keep.tile([P, 2, CW, T], BF16, align_bytes=64)
+        pair_sb[CHUNKS - 2] = pair_last
+        gain_x(2, nc.gpsimd, range(4))
+
+        for s in range(CHUNKS):
             early = s < 2
-            if s + 4 < CHUNKS:
+            if s + 4 < CHUNKS - 1:
                 load_x(s + 4)
+            if s == 0:
+                stage_q(s)
+                stage_b(s)
+                interleave(s)
             quantize(s)
             if s >= 1:
-                product(yq[s - 1], p2, s - 1)
-            if s < CHUNKS:
+                product(yq[s - 1], p2, s - 1, "second")
+            if s >= 2:
+                nc.gpsimd.tensor_copy(out=gate[:], in_=code_sb[s])
+            if s >= 1:
                 stage_q(s)
-                if 4 <= s + 2 < CHUNKS:
-                    gain_x_out(s + 2)
-            if s + 1 < CHUNKS:
-                scale_r(s + 1, range(T) if early else range(R_ACT), False)
-                scale_r(s + 1, range(0) if early else range(R_ACT, T), True)
-            if s < CHUNKS:
-                stage_pool_w(s)
+            if s + 2 in PE_CHUNKS:
+                gain_x_out(s + 2)
             if s + 1 < CHUNKS and not early:
-                scale_cx(s + 1, range(T), True)
-            if s == 0:
-                gain_x(3, nc.gpsimd)
-            if s < CHUNKS:
+                scale_r(s + 1, range(2, R_ACT), False)
+                scale_r(s + 1, range(R_ACT, T), True)
+            if s == 1:
+                gain_x(3, nc.gpsimd, range(4))
+            if s == 2:
+                scale_cx(s, (3, 2, 0, 1), True)
+            stage_pool_w(s)
+            if s + 1 < CHUNKS and not early:
+                scale_cx(s + 1, (3, 2, 0, 1), True)
+            if 4 <= s < 8:
+                gain_x(CHUNKS - 1, nc.gpsimd, (s - 4,))
+            if s >= 1:
                 stage_b(s)
                 interleave(s)
             if s + 1 < CHUNKS and early:
-                scale_cx(s + 1, range(T), False)
+                scale_r(s + 1, range(T), False)
+                if s == 0:
+                    scale_cx(s + 1, range(T), False)
+            if s + 1 < CHUNKS and not early:
+                scale_r(s + 1, (1, 0), False)
             if s >= 1:
                 stage_d(s - 1)
-            if 4 <= s + 3 < CHUNKS:
+            if s + 3 in PE_CHUNKS and s >= 1:
                 gain_x_pe(s + 3)
-            if s < CHUNKS:
-                stage_w(s)
+            if s == CHUNKS - 1:
+                quantize(s + 1)
+                product(yq[s], p2, s, "second")
+            stage_w(s)
             if s + 1 < CHUNKS:
-                product(xq[s + 1], p1, s + 1)
+                product(xq[s + 1], p1, s + 1, "first")
+        stage_d(CHUNKS - 1)

@@ -8,7 +8,7 @@ P = 128
 T = 4
 CW = 512
 CHUNKS = C // CW
-POOL_W = (1, 2)
+POOL_W = 1
 R_ACT = 3
 PE_CHUNKS = (1,) + tuple(range(4, 15))
 
@@ -110,7 +110,7 @@ def tile_chebyshevfilteredsubspaceblock_t_kernel(tc, h_bytes, h_scale, g, v, x, 
             banks = []
             for i in range(2):
                 cols = slice(i * CW // 2, (i + 1) * CW // 2)
-                bank = psum.tile([P, T, CW // 2], BF16, name=f"second_{i}")
+                bank = psum.tile([P, T, CW // 2], BF16, name=f"second_{1 - i}")
                 for t in range(T):
                     nc.tensor.matmul(out=bank[:, t, :], lhsT=diag[:, t, :], rhs=x_sb[c][:, t, cols], start=True, stop=True)
                 banks.append(bank)
@@ -181,27 +181,27 @@ def tile_chebyshevfilteredsubspaceblock_t_kernel(tc, h_bytes, h_scale, g, v, x, 
 
         def stage_w(c):
             w = w_sb[c]
-            for t in reversed(range(T - POOL_W[c % 2])):
+            for t in range(T - POOL_W):
                 nc.vector.scalar_tensor_tensor(
                     out=w[:, t, :], in0=p1[c][t][:], scalar=bau[:, t:t + 1], in1=cx_sb[c][:, t, :], op0=MULT, op1=ADD)
 
         def stage_q(c):
             w = two.tile([P, T, CW], F32)
             w_sb[c] = w
-            q = two.tile([P, POOL_W[c % 2], CW], F32)
+            q = two.tile([P, POOL_W, CW], F32)
             q_sb[c] = q
-            for j in reversed(range(POOL_W[c % 2])):
-                t = T - POOL_W[c % 2] + j
+            for j in reversed(range(POOL_W)):
+                t = T - POOL_W + j
                 nc.scalar.activation(out=q[:, j, :], in_=p1[c][t][:], func=ACT_COPY, scale=bau[:, t:t + 1])
 
         def stage_pool_w(c):
-            for j in reversed(range(POOL_W[c % 2])):
-                t = T - POOL_W[c % 2] + j
+            for j in reversed(range(POOL_W)):
+                t = T - POOL_W + j
                 nc.gpsimd.tensor_tensor(out=w_sb[c][:, t, :], in0=q_sb[c][:, j, :], in1=cx_sb[c][:, t, :], op=ADD)
 
         def stage_d(c):
             o = three.tile([P, T, CW], F32)
-            for t in range(T):
+            for t in reversed(range(T)):
                 nc.vector.scalar_tensor_tensor(
                     out=o[:, t, :], in0=p2[c][t][:], scalar=B, in1=w_sb[c][:, t, :], op0=MULT, op1=ADD)
                 if c == CHUNKS - 1:
@@ -210,9 +210,7 @@ def tile_chebyshevfilteredsubspaceblock_t_kernel(tc, h_bytes, h_scale, g, v, x, 
                 nc.sync.dma_start(out=out_view[:, :, c * CW:(c + 1) * CW], in_=o[:])
 
         def interleave(c):
-            nc.scalar.copy(
-                out=pair_of(c + 1)[:, 1].rearrange("p (n i) t -> p n t i", i=4),
-                in_=yg_sb[c][:].rearrange("p t (n i) -> p n t i", i=4))
+            nc.scalar.copy(out=pair_of(c + 1)[:, 1], in_=yg_sb[c][:].rearrange("p t n -> p n t"))
 
         gate = keep.tile([P, 1], U32)
         diag = keep.tile([P, T, P], BF16)
@@ -261,15 +259,13 @@ def tile_chebyshevfilteredsubspaceblock_t_kernel(tc, h_bytes, h_scale, g, v, x, 
             quantize(s)
             if s >= 1:
                 product(yq[s - 1], p2, s - 1, "second")
-            if s >= 2:
-                nc.gpsimd.tensor_copy(out=gate[:], in_=code_sb[s])
             if s >= 1:
                 stage_q(s)
+            if s + 1 < CHUNKS and not early:
+                scale_r(s + 1, range(R_ACT), False)
+                scale_r(s + 1, range(R_ACT, T), True)
             if s + 2 in PE_CHUNKS:
                 gain_x_out(s + 2)
-            if s + 1 < CHUNKS and not early:
-                scale_r(s + 1, range(2, R_ACT), False)
-                scale_r(s + 1, range(R_ACT, T), True)
             if s == 1:
                 gain_x(3, nc.gpsimd, range(4))
             if s == 2:
@@ -286,8 +282,9 @@ def tile_chebyshevfilteredsubspaceblock_t_kernel(tc, h_bytes, h_scale, g, v, x, 
                 scale_r(s + 1, range(T), False)
                 if s == 0:
                     scale_cx(s + 1, range(T), False)
-            if s + 1 < CHUNKS and not early:
-                scale_r(s + 1, (1, 0), False)
+            if s < CHUNKS - 1:
+                stage_w(s)
+                product(xq[s + 1], p1, s + 1, "first")
             if s >= 1:
                 stage_d(s - 1)
             if s + 3 in PE_CHUNKS and s >= 1:
@@ -295,7 +292,5 @@ def tile_chebyshevfilteredsubspaceblock_t_kernel(tc, h_bytes, h_scale, g, v, x, 
             if s == CHUNKS - 1:
                 quantize(s + 1)
                 product(yq[s], p2, s, "second")
-            stage_w(s)
-            if s + 1 < CHUNKS:
-                product(xq[s + 1], p1, s + 1, "first")
+                stage_w(s)
         stage_d(CHUNKS - 1)

from contextlib import ExitStack

import concourse.mybir as mybir
from concourse.masks import make_identity

N, C = 512, 8192
P = 128
T = 4
CW = 512
CHUNKS = C // CW
POOL_W = 1
R_ACT = 3
PE_CHUNKS = (1,) + tuple(range(4, 15))

F32 = mybir.dt.float32
BF16 = mybir.dt.bfloat16
U32 = mybir.dt.uint32
U8 = mybir.dt.uint8
FP8 = mybir.dt.float8_e4m3fn
FP8X4 = mybir.dt.float8_e4m3fn_x4
ADD = mybir.AluOpType.add
MULT = mybir.AluOpType.mult
ACT_COPY = mybir.ActivationFunctionType.Copy

CC = 0.75
E = 1.75
A0 = -2.3
S1 = E / (A0 - CC)
S2 = 1.0 / (2.0 / S1 - S1)
A = S1 / E
B = 2.0 * S2 / E

FLOPS = 2 * 2 * N * N * C


def tile_chebyshevfilteredsubspaceblock_t_kernel(tc, h_bytes, h_scale, g, v, x, out):
    nc = tc.nc
    x_view = x.rearrange("(p t) n -> p t n", t=T)
    out_view = out.rearrange("(p t) n -> p t n", t=T)

    with ExitStack() as ctx:
        keep = ctx.enter_context(tc.tile_pool(name="keep", bufs=1))
        xs = ctx.enter_context(tc.tile_pool(name="xs", bufs=5))
        two = ctx.enter_context(tc.tile_pool(name="two", bufs=2))
        four = ctx.enter_context(tc.tile_pool(name="four", bufs=4))
        three = ctx.enter_context(tc.tile_pool(name="three", bufs=3))
        psum = ctx.enter_context(tc.psum_pool(name="psum", bufs=1))

        x_sb, pair_sb, xq, r_sb, cx_sb, p1, w_sb, yg_sb, yq, p2, q_sb, xg_ps, code_sb = ({} for i in range(13))

        def load_x(c):
            xt = xs.tile([P, T, CW], BF16)
            nc.sync.dma_start(out=xt[:], in_=x_view[:, :, c * CW:(c + 1) * CW])
            x_sb[c] = xt

        def load_last():
            x_last = keep.tile([P, T, CW], BF16)
            nc.sync.dma_start(out=x_last[:], in_=x_view[:, :, C - CW:])
            x_sb[CHUNKS - 1] = x_last

        ctx.enter_context(tc.manual_schedule())

        sc = keep.tile([P, N], F32)
        nc.scalar.dma_start(out=sc[:], in_=h_scale.rearrange("o k -> (o k)").partition_broadcast(P))
        gb = keep.tile([P, T], BF16)
        vb = keep.tile([P, T], BF16)
        nc.sync.dma_start(out=gb[:], in_=g.rearrange("(p t) -> p t", t=T))
        nc.sync.dma_start(out=vb[:], in_=v.rearrange("(p t) -> p t", t=T))
        load_x(0)
        hb = keep.tile([P, T, N], U8)
        nc.sync.dma_start(out=hb[:], in_=h_bytes.rearrange("(m t) k -> m t k", t=T))
        for c in range(1, 4):
            load_x(c)
        load_last()

        ident = keep.tile([P, P], F32)
        make_identity(nc, ident[:])

        u = keep.tile([P, T], F32)
        ga = keep.tile([P, T], F32)
        gau = keep.tile([P, T], F32)
        bau = keep.tile([P, T], F32)
        cxv = keep.tile([P, T], F32)
        tmp = keep.tile([P, T], F32)
        nc.vector.tensor_scalar(out=u[:], in0=vb[:], scalar1=-CC, scalar2=None, op0=ADD)
        nc.vector.tensor_scalar(out=ga[:], in0=gb[:], scalar1=A, scalar2=None, op0=MULT)
        nc.vector.tensor_scalar(out=bau[:], in0=u[:], scalar1=A * B, scalar2=None, op0=MULT)
        nc.vector.tensor_tensor(out=gau[:], in0=ga[:], in1=u[:], op=MULT)
        nc.vector.tensor_tensor(out=tmp[:], in0=bau[:], in1=u[:], op=MULT)
        nc.vector.tensor_scalar(out=cxv[:], in0=tmp[:], scalar1=-S1 * S2, scalar2=None, op0=ADD)

        def pair_of(s):
            if s not in pair_sb:
                pair = four.tile([P, 2, CW, T], BF16, align_bytes=64)
                pair_sb[s] = pair
            return pair_sb[s]

        def gain_x(c, engine, pieces):
            pair = pair_of(c - 1)
            for i in pieces:
                cols = slice(i * CW // 4, (i + 1) * CW // 4)
                engine.tensor_tensor(
                    out=pair[:, 0, cols, :],
                    in0=x_sb[c][:, :, cols].rearrange("p t n -> p n t"),
                    in1=gb[:].unsqueeze(1).to_broadcast([P, CW // 4, T]),
                    op=MULT,
                )

        def gain_x_pe(c):
            banks = []
            for i in range(2):
                cols = slice(i * CW // 2, (i + 1) * CW // 2)
                bank = psum.tile([P, T, CW // 2], BF16, name=f"second_{1 - i}")
                for t in range(T):
                    nc.tensor.matmul(out=bank[:, t, :], lhsT=diag[:, t, :], rhs=x_sb[c][:, t, cols], start=True, stop=True)
                banks.append(bank)
            xg_ps[c] = banks

        def gain_x_out(c):
            pair = pair_of(c - 1)
            for i in range(2):
                cols = slice(i * CW // 2, (i + 1) * CW // 2)
                nc.scalar.copy(out=pair[:, 0, cols, :], in_=xg_ps[c][i][:].rearrange("p t n -> p n t"))

        def quantize(s):
            codes = two.tile([P, 2, CW], U32, align_bytes=64)
            scales = two.tile([P, 2, CW], U8, align_bytes=64)
            lo = 0 if s + 1 < CHUNKS else 1
            hi = 2 if s >= 1 else 1
            nc.vector.quantize_mx(
                out=codes[:, lo:hi, :].rearrange("p h n -> p (h n)").bitcast(FP8X4),
                scales=scales[:, lo:hi, :].rearrange("p h n -> p (h n)"),
                in_=pair_sb[s][:, lo:hi].rearrange("p h n t -> p (h n t)"))
            code_sb[s] = codes[:, lo, 0:1]
            xq[s + 1] = codes[:, 0, :], scales[:, 0, :]
            yq[s - 1] = codes[:, 1, :], scales[:, 1, :]

        def times_x(out_ap, c, t, factor, on_pool):
            if on_pool:
                nc.gpsimd.tensor_scalar(out=out_ap, in0=x_sb[c][:, t, :], scalar1=factor[:, t:t + 1], scalar2=0.0, op0=MULT, op1=ADD)
            else:
                nc.scalar.activation(out=out_ap, in_=x_sb[c][:, t, :], func=ACT_COPY, scale=factor[:, t:t + 1])

        def scale_r(c, ts, on_pool):
            if c not in r_sb:
                r = two.tile([P, T, CW], F32)
                r_sb[c] = r
            for t in ts:
                times_x(r_sb[c][:, t, :], c, t, gau, on_pool)

        def scale_cx(c, ts, on_pool):
            if c not in cx_sb:
                cx = two.tile([P, T, CW], F32)
                cx_sb[c] = cx
            for t in ts:
                times_x(cx_sb[c][:, t, :], c, t, cxv, on_pool)

        def product(q, p_dict, c, kind):
            codes, scales = q
            res = {}
            for t in reversed(range(T)):
                acc = psum.tile([P, CW], F32, name=f"{kind}_{t}")
                nc.tensor.matmul_mx(
                    out=acc[:],
                    lhsT=h_codes[:, t * P:(t + 1) * P].bitcast(FP8X4),
                    lhsT_scale=h_scales[:, t * P:(t + 1) * P],
                    rhs=codes.bitcast(FP8X4),
                    rhs_scale=scales,
                    start=True,
                    stop=True,
                )
                res[t] = acc
            p_dict[c] = res

        def stage_b(c):
            yg = two.tile([P, T, CW], BF16)
            for t in range(T):
                nc.vector.scalar_tensor_tensor(
                    out=yg[:, t, :], in0=p1[c][t][:], scalar=ga[:, t:t + 1], in1=r_sb[c][:, t, :], op0=MULT, op1=ADD)
            yg_sb[c] = yg

        def stage_w(c):
            w = w_sb[c]
            for t in range(T - POOL_W):
                nc.vector.scalar_tensor_tensor(
                    out=w[:, t, :], in0=p1[c][t][:], scalar=bau[:, t:t + 1], in1=cx_sb[c][:, t, :], op0=MULT, op1=ADD)

        def stage_q(c):
            w = two.tile([P, T, CW], F32)
            w_sb[c] = w
            q = two.tile([P, POOL_W, CW], F32)
            q_sb[c] = q
            for j in reversed(range(POOL_W)):
                t = T - POOL_W + j
                nc.scalar.activation(out=q[:, j, :], in_=p1[c][t][:], func=ACT_COPY, scale=bau[:, t:t + 1])

        def stage_pool_w(c):
            for j in reversed(range(POOL_W)):
                t = T - POOL_W + j
                nc.gpsimd.tensor_tensor(out=w_sb[c][:, t, :], in0=q_sb[c][:, j, :], in1=cx_sb[c][:, t, :], op=ADD)

        def stage_d(c):
            o = three.tile([P, T, CW], F32)
            for t in reversed(range(T)):
                nc.vector.scalar_tensor_tensor(
                    out=o[:, t, :], in0=p2[c][t][:], scalar=B, in1=w_sb[c][:, t, :], op0=MULT, op1=ADD)
                if c == CHUNKS - 1:
                    nc.sync.dma_start(out=out_view[:, t:t + 1, c * CW:(c + 1) * CW], in_=o[:, t:t + 1, :])
            if c < CHUNKS - 1:
                nc.sync.dma_start(out=out_view[:, :, c * CW:(c + 1) * CW], in_=o[:])

        def interleave(c):
            nc.scalar.copy(out=pair_of(c + 1)[:, 1], in_=yg_sb[c][:].rearrange("p t n -> p n t"))

        gate = keep.tile([P, 1], U32)
        diag = keep.tile([P, T, P], BF16)
        gain_x(0, nc.vector, range(4))
        hf = keep.tile([P, T, N], BF16, align_bytes=64)
        for t in range(T):
            nc.vector.tensor_tensor(out=hf[:, t, :], in0=hb[:, t, :].bitcast(FP8), in1=sc[:], op=MULT)
        for t in range(T):
            nc.vector.tensor_scalar(out=diag[:, t, :], in0=ident[:], scalar1=gb[:, t:t + 1], scalar2=None, op0=MULT)
        quantize(-1)
        scale_r(0, range(T), False)
        hg = keep.tile([P, N, T], BF16, align_bytes=64)
        hg_words = hg[:].rearrange("p n t -> p (n t)").bitcast(F32).rearrange("p (t m u) -> p t m u", t=T, u=2)
        for i in range(2):
            turned = psum.tile([P, CW], F32, name=f"second_{i + 2}")
            bank = turned[:].rearrange("p (t u m) -> p t u m", t=2, u=2)
            for j in range(2):
                words = hf[:, 2 * i + j, :].bitcast(F32)
                for k in range(2):
                    nc.tensor.transpose(bank[:, j, k, :], words[:, k::2], ident[:])
            if i == 0:
                nc.vector.tensor_copy(out=hg_words[:, 2 * i:2 * i + 2], in_=bank.rearrange("p t u m -> p t m u"))
            else:
                nc.scalar.copy(out=hg_words[:, 2 * i:2 * i + 2], in_=bank.rearrange("p t u m -> p t m u"))
        h_codes = keep.tile([P, N], U32, align_bytes=64)
        h_scales = keep.tile([P, N], U8, align_bytes=64)
        nc.vector.quantize_mx(out=h_codes[:].bitcast(FP8X4), scales=h_scales[:], in_=hg[:].rearrange("p n t -> p (n t)"))
        gain_x_pe(1)
        product(xq[0], p1, 0, "first")
        gain_x_out(1)
        scale_cx(0, range(T), False)
        nc.gpsimd.tensor_copy(out=gate[:], in_=h_codes[:, 0:1])

        pair_last = keep.tile([P, 2, CW, T], BF16, align_bytes=64)
        pair_sb[CHUNKS - 2] = pair_last
        gain_x(2, nc.gpsimd, range(4))

        for s in range(CHUNKS):
            early = s < 2
            if s + 4 < CHUNKS - 1:
                load_x(s + 4)
            if s == 0:
                stage_q(s)
                stage_b(s)
                interleave(s)
            quantize(s)
            if s >= 1:
                product(yq[s - 1], p2, s - 1, "second")
            if s >= 1:
                stage_q(s)
            if s + 1 < CHUNKS and not early:
                scale_r(s + 1, range(R_ACT), False)
                scale_r(s + 1, range(R_ACT, T), True)
            if s + 2 in PE_CHUNKS:
                gain_x_out(s + 2)
            if s == 1:
                gain_x(3, nc.gpsimd, range(4))
            if s == 2:
                scale_cx(s, (3, 2, 0, 1), True)
            stage_pool_w(s)
            if s + 1 < CHUNKS and not early:
                scale_cx(s + 1, (3, 2, 0, 1), True)
            if 4 <= s < 8:
                gain_x(CHUNKS - 1, nc.gpsimd, (s - 4,))
            if s >= 1:
                stage_b(s)
                interleave(s)
            if s + 1 < CHUNKS and early:
                scale_r(s + 1, range(T), False)
                if s == 0:
                    scale_cx(s + 1, range(T), False)
            if s < CHUNKS - 1:
                stage_w(s)
                product(xq[s + 1], p1, s + 1, "first")
            if s >= 1:
                stage_d(s - 1)
            if s + 3 in PE_CHUNKS and s >= 1:
                gain_x_pe(s + 3)
            if s == CHUNKS - 1:
                quantize(s + 1)
                product(yq[s], p2, s, "second")
                stage_w(s)
        stage_d(CHUNKS - 1)
